import numpy as np
import ml_dtypes


def mxq(x, axis, fmt="e4m3"):
    dtype, down = {"e4m3": (ml_dtypes.float8_e4m3fn, 7), "e5m2": (ml_dtypes.float8_e5m2, 14)}[fmt]
    v = np.moveaxis(np.asarray(x, np.float32).astype(ml_dtypes.bfloat16).astype(np.float64), axis, -1)
    blocks = v.reshape(v.shape[:-1] + (-1, 32))
    amax = np.abs(blocks).max(-1, keepdims=True)
    byte = np.maximum(np.where(amax > 0, np.frexp(amax)[1] - 1 + 127, 0) - down, 1)
    scale = np.exp2(byte - 127.0)
    codes = (blocks / scale).astype(np.float32).astype(dtype).astype(np.float64)
    return np.moveaxis((codes * scale).reshape(v.shape), -1, axis)


WIDE = False


def mx_kscale(k):
    if not WIDE:
        return np.ones(k)
    levels = np.array([10, -10, 5, -5, 0])
    if k % 512:
        return np.exp2(np.random.permutation(np.resize(levels, k // 32))).repeat(32)
    a = np.empty((k // 512, 16))
    for p in range(k // 512):
        a[p, :8] = np.random.permutation(np.resize(levels, 8))
        for g in range(8):
            far = levels[np.abs(levels - a[p, g]) >= 10]
            a[p, g + 8] = far[np.random.randint(len(far))]
    return np.exp2(a.ravel()).repeat(32)


def f64(x):
    return np.asarray(x).astype(np.float64)


E2M1 = np.array([0.0, 0.5, 1.0, 1.5, 2.0, 3.0, 4.0, 6.0, -0.0, -0.5, -1.0, -1.5, -2.0, -3.0, -4.0, -6.0])


def pack_weight(w, fmt):
    k, n = w.shape
    w = f64(np.asarray(w, np.float32).astype(ml_dtypes.bfloat16)).reshape(k // 32, 32, n)
    amax = np.abs(w).max(1)
    if fmt == "e4m3":
        byte = np.frexp(amax)[1] - 1 + 127 - 7
    else:
        mant, ex = np.frexp(amax / 6.0)
        byte = np.where(mant > 0.5, ex, ex - 1) + 127
    byte = np.clip(np.where(amax > 0, byte, 1), 1, 254)
    scaled = (w * np.exp2(127.0 - byte)[:, None, :]).reshape(k, n).astype(np.float32)
    by_word = np.ascontiguousarray(scaled.reshape(k // 512, 128, 4, n).transpose(0, 1, 3, 2))
    if fmt == "e4m3":
        words = by_word.astype(ml_dtypes.float8_e4m3fn).view(np.uint8)
    else:
        c = by_word.astype(ml_dtypes.float4_e2m1fn).view(np.uint8) & 0xF
        words = (c[..., 0::2] | (c[..., 1::2] << 4)).reshape(k // 512, 128, 2 * n)
    return np.ascontiguousarray(words), np.ascontiguousarray(byte.astype(np.uint8).reshape(k // 512, 16, n))


def unpack_weight(words, scales, fmt):
    g, _, n = scales.shape
    words = np.ascontiguousarray(words).reshape(g, 128, n, -1)
    if fmt == "e4m3":
        vals = words.view(ml_dtypes.float8_e4m3fn).astype(np.float64)
    else:
        nib = np.empty((g, 128, n, 4), np.uint8)
        nib[..., 0::2] = words & 0xF
        nib[..., 1::2] = words >> 4
        vals = E2M1[nib]
    vals = vals * np.repeat(np.exp2(scales.astype(np.float64) - 127.0), 8, axis=1)[..., None]
    return vals.transpose(0, 1, 3, 2).reshape(g * 512, n)


K, L, T, R, N = 1024, 512, 512, 512, 512


def setup_inputs():
    n = np.random.standard_normal
    fk = mx_kscale(K)
    fr = mx_kscale(R)
    fl = mx_kscale(L)
    xtp = pack_weight(n((K, T)) / fk[:, None], "e4m3")
    wap = pack_weight(n((K, R)) * 1 / np.sqrt(K) * fk[:, None] * fr, "e2m1")
    xqp = pack_weight(n((L, T)) / fl[:, None], "e4m3")
    wcp = pack_weight(n((L, R)) * 1 / np.sqrt(L) * fl[:, None] * fr, "e2m1")
    wbp = pack_weight(n((R, N)) * 1 / np.sqrt(R) / fr[:, None], "e4m3")
    return {
        "xt_words": xtp[0],
        "xt_scales": xtp[1],
        "wa_words": wap[0],
        "wa_scales": wap[1],
        "xq_words": xqp[0],
        "xq_scales": xqp[1],
        "wc_words": wcp[0],
        "wc_scales": wcp[1],
        "wb_words": wbp[0],
        "wb_scales": wbp[1],
        "b": (np.random.uniform(-0.5, 0.5, (N, 1))).astype(np.float32),
    }


def reference(xt_words, xt_scales, wa_words, wa_scales, xq_words, xq_scales, wc_words, wc_scales, wb_words, wb_scales, b):
    xtu = unpack_weight(xt_words, xt_scales, "e4m3")
    wau = unpack_weight(wa_words, wa_scales, "e2m1")
    xqu = unpack_weight(xq_words, xq_scales, "e4m3")
    wcu = unpack_weight(wc_words, wc_scales, "e2m1")
    wbu = unpack_weight(wb_words, wb_scales, "e4m3")
    z = wau.T @ xtu + wcu.T @ xqu
    z1 = np.pad(z, ((0, 0), (1, 0)))[:, :T]
    z2 = np.pad(z, ((0, 0), (2, 0)))[:, :T]
    hid = np.maximum(z + 0.5 * z1 + 0.25 * z2, 0.0)
    hidq = mxq(hid, 0, "e4m3")
    p = wbu.T @ hidq
    y = p + f64(b)
    return y

@@ -1,0 +1,246 @@
+from contextlib import ExitStack
+
+import concourse.mybir as mybir
+
+K, L, T, R, N = 1024, 512, 512, 512, 512
+FLOPS = 2 * (K + L) * R * T + 2 * R * N * T
+
+F32 = mybir.dt.float32
+BF16 = mybir.dt.bfloat16
+I32 = mybir.dt.int32
+U16 = mybir.dt.uint16
+U8 = mybir.dt.uint8
+FP8X4 = mybir.dt.float8_e4m3fn_x4
+FP4X4 = mybir.dt.float4_e2m1fn_x4
+ALU = mybir.AluOpType
+ACT = mybir.ActivationFunctionType
+
+P = 128
+PACK = 4
+TC = 128
+CHUNKS = T // TC
+PASSES = 3
+
+
+def load_scale_rows(queue, plane, scales, rows):
+    z = scales.shape[0]
+    src = scales.bitcast(I32).rearrange("z (q r) c -> r q z c", r=4)
+    dst = plane.bitcast(I32).rearrange("p (z c) -> p z c", z=z)
+    for r in rows:
+        queue.dma_start(out=dst[r:P:32], in_=src[r])
+
+
+def tile_mix_momentum_of_two_inputs_kernel(
+    tc, xt_words, xt_scales, wa_words, wa_scales, xq_words, xq_scales,
+    wc_words, wc_scales, wb_words, wb_scales, b, out,
+):
+    nc = tc.nc
+    with ExitStack() as ctx:
+        sb = ctx.enter_context(tc.tile_pool(name="sb", bufs=1))
+        ps = ctx.enter_context(tc.psum_pool(name="ps", bufs=1))
+        ctx.enter_context(tc.manual_schedule())
+
+        wa_raw = sb.tile([P, 2 * 2 * R], U8, align_bytes=64)
+        wc_raw = sb.tile([P, 2 * R], U8, align_bytes=64)
+        ws_raw = sb.tile([P, PASSES * R], U8, align_bytes=64)
+        xts = sb.tile([P, 2 * T], U8, align_bytes=64)
+        xqs = sb.tile([P, T], U8, align_bytes=64)
+        wbs = sb.tile([P, N], U8, align_bytes=64)
+        xt = sb.tile([P, 2 * T], I32, align_bytes=64)
+        xq = sb.tile([P, T], I32, align_bytes=64)
+        wb = sb.tile([P, N], I32, align_bytes=64)
+        bias = sb.tile([P, N // P], F32, align_bytes=64)
+        w_perm = [sb.tile([P, 2 * R], U8, align_bytes=64, name="w_perm%d" % g) for g in range(PASSES)]
+        ws_perm = [sb.tile([P, R], U8, align_bytes=64, name="ws_perm%d" % g) for g in range(PASSES)]
+        zs = sb.tile([P, PACK * (T + 1)], F32, align_bytes=64)
+        ws = sb.tile([P, PACK * (T + 1)], F32, align_bytes=64)
+        warm = sb.tile([P, 8], F32, align_bytes=64)
+
+        nc.vector.memset(ws_raw[:].bitcast(I32), 0)
+        nc.gpsimd.memset(xqs[:].bitcast(I32), 0)
+        nc.vector.memset(xts[:].bitcast(I32), 0)
+        nc.vector.memset(wbs[:].bitcast(I32), 0)
+        nc.vector.memset(zs[:, 0:PACK], 0.0)
+        nc.vector.memset(ws[:, 0:PACK], 0.0)
+        nc.vector.memset(warm[:], 0.0)
+
+        ones = sb.tile([P, PACK * TC], BF16, align_bytes=64)
+        ones_q = sb.tile([P, TC], I32, align_bytes=64)
+        ones_s = sb.tile([P, TC], U8, align_bytes=64)
+        nc.vector.memset(ones[:], 1.0)
+        nc.vector.quantize_mx(out=ones_q[:].bitcast(FP8X4), scales=ones_s[:], in_=ones[:])
+        warm_bank = ps.tile([P, 2 * TC], F32, name="warm_bank", tag="y1_1")
+        for i in range(24):
+            nc.tensor.matmul_mx(out=warm_bank[:, (i % 2) * TC:(i % 2 + 1) * TC], lhsT=ones_q[:].bitcast(FP8X4), lhsT_scale=ones_s[:],
+                                rhs=ones_q[:].bitcast(FP8X4), rhs_scale=ones_s[:], start=True, stop=True)
+
+        def load_words(queue, dst, src):
+            z = src.shape[0]
+            queue.dma_start(out=dst.bitcast(I32).rearrange("p (z c) -> p z c", z=z),
+                            in_=src.bitcast(I32).rearrange("z p c -> p z c"))
+
+        def fp8_rows(words):
+            return words.rearrange("z p c t -> z p (c t)")
+
+        load_scale_rows(nc.gpsimd, xqs[:], xq_scales, range(4))
+        load_words(nc.sync, wa_raw[:], wa_words)
+        load_scale_rows(nc.scalar, ws_raw[:, 0:2 * R], wa_scales, range(4))
+        load_words(nc.sync, wc_raw[:], wc_words)
+        load_scale_rows(nc.scalar, ws_raw[:, 2 * R:3 * R], wc_scales, range(0, 2))
+        load_words(nc.sync, xt[:], fp8_rows(xt_words))
+        load_scale_rows(nc.scalar, ws_raw[:, 2 * R:3 * R], wc_scales, range(2, 4))
+        load_scale_rows(nc.scalar, xts[:], xt_scales, range(0, 2))
+        load_words(nc.sync, xq[:], fp8_rows(xq_words))
+        load_scale_rows(nc.sync, xts[:], xt_scales, range(2, 4))
+        load_words(nc.sync, wb[:], fp8_rows(wb_words))
+        load_scale_rows(nc.sync, wbs[:], wb_scales, range(4))
+        with nc.allow_non_contiguous_dma(reason="one bias value a partition"):
+            nc.sync.dma_start(out=bias[:], in_=b.rearrange("(i p) o -> p (i o)", p=P))
+
+        nc.scalar.activation(out=warm[:, 4:5], in_=warm[:, 0:1], func=ACT.Relu)
+
+        raw_words = [wa_raw[:, 0:2 * R], wa_raw[:, 2 * R:4 * R], wc_raw[:]]
+        x_words = [xt[:, 0:T], xt[:, T:2 * T], xq[:]]
+
+        x_scales = [xts[:, 0:T], xts[:, T:2 * T], xqs[:]]
+
+        def permute(g):
+            nc.vector.tensor_copy(
+                out=w_perm[g][:].bitcast(U16).rearrange("p (j m) -> p j m", j=PACK),
+                in_=raw_words[g].bitcast(U16).rearrange("p (m j) -> p j m", j=PACK))
+            nc.vector.tensor_copy(
+                out=ws_perm[g][:].rearrange("p (j m) -> p j m", j=PACK),
+                in_=ws_raw[:, g * R:(g + 1) * R].rearrange("p (m j) -> p j m", j=PACK))
+
+        z_bank = [ps.tile([P, PACK * TC], F32, name="z_bank%d" % c) for c in range(CHUNKS)]
+
+        def first_layer(g, c):
+            for j in range(PACK):
+                nc.tensor.matmul_mx(
+                    out=z_bank[c][:, j * TC:(j + 1) * TC],
+                    lhsT=w_perm[g][:, 2 * P * j:2 * P * (j + 1)].bitcast(FP4X4),
+                    lhsT_scale=ws_perm[g][:, P * j:P * (j + 1)],
+                    rhs=x_words[g][:, c * TC:(c + 1) * TC].bitcast(FP8X4),
+                    rhs_scale=x_scales[g][:, c * TC:(c + 1) * TC],
+                    start=(g == 0 and j == 0),
+                    stop=(g == PASSES - 1 and j == PACK - 1),
+                )
+
+        W = PACK * TC
+        h32 = [sb.tile([P, W], F32, align_bytes=64, name="h32_%d" % c) for c in range(CHUNKS)]
+        h16 = [sb.tile([P, W], BF16, align_bytes=64, name="h16_%d" % c) for c in range(CHUNKS)]
+        hq = [sb.tile([P, TC], I32, align_bytes=64, name="hq%d" % c) for c in range(CHUNKS)]
+        hs = [sb.tile([P, TC], U8, align_bytes=64, name="hs%d" % c) for c in range(CHUNKS)]
+        res = [sb.tile([P, W], F32, align_bytes=64, name="res%d" % c) for c in range(CHUNKS)]
+        y_bank = {}
+
+        def now(c):
+            return slice(PACK + c * W, PACK + (c + 1) * W)
+
+        def before(c):
+            return slice(c * W, (c + 1) * W)
+
+        def copy_z(c):
+            nc.scalar.copy(out=zs[:, now(c)].rearrange("p (t j) -> p t j", j=PACK),
+                           in_=z_bank[c][:].rearrange("p (j t) -> p t j", j=PACK))
+
+        def fir1(c):
+            nc.vector.scalar_tensor_tensor(out=ws[:, now(c)], in0=zs[:, before(c)], scalar=0.5,
+                                           in1=zs[:, now(c)], op0=ALU.mult, op1=ALU.add)
+
+        def fir2(c):
+            nc.vector.scalar_tensor_tensor(out=h32[c][:], in0=ws[:, before(c)], scalar=0.5,
+                                           in1=zs[:, now(c)], op0=ALU.mult, op1=ALU.add)
+
+        def relu_s(c):
+            nc.scalar.activation(out=h16[c][:], in_=h32[c][:], func=ACT.Relu)
+
+        def relu_v(c):
+            nc.vector.tensor_scalar(out=h16[c][:], in0=h32[c][:], scalar1=0.0, scalar2=None, op0=ALU.max)
+
+        def quant(c):
+            nc.vector.quantize_mx(out=hq[c][:].bitcast(FP8X4), scales=hs[c][:], in_=h16[c][:])
+
+        def second_layer(c):
+            for half in range(2):
+                bank = ps.tile([P, 2 * TC], F32, name="y%d_%d" % (c, half), tag="y%d_%d" % (c % 2, half))
+                y_bank[c, half] = bank
+                for i in range(2):
+                    n0 = (2 * half + i) * P
+                    nc.tensor.matmul_mx(
+                        out=bank[:, i * TC:(i + 1) * TC],
+                        lhsT=wb[:, n0:n0 + P].bitcast(FP8X4), lhsT_scale=wbs[:, n0:n0 + P],
+                        rhs=hq[c][:].bitcast(FP8X4), rhs_scale=hs[c][:],
+                        start=True, stop=True)
+
+        def bias_s(c, half):
+            for i in range(2):
+                k = 2 * half + i
+                nc.scalar.activation(out=res[c][:, k * TC:(k + 1) * TC], in_=y_bank[c, half][:, i * TC:(i + 1) * TC],
+                                     func=ACT.Identity, bias=bias[:, k:k + 1])
+
+        def bias_v(c, half):
+            nc.vector.tensor_tensor(
+                out=res[c][:, 2 * half * TC:2 * (half + 1) * TC].rearrange("p (i t) -> p i t", i=2),
+                in0=y_bank[c, half][:].rearrange("p (i t) -> p i t", i=2),
+                in1=bias[:, 2 * half:2 * half + 2].unsqueeze(2).to_broadcast([P, 2, TC]),
+                op=ALU.add)
+
+        out_v = out.rearrange("(i p) t -> p i t", p=P)
+
+        def store(c, lo, hi, queue):
+            queue.dma_start(out=out_v[:, lo:hi, c * TC:(c + 1) * TC],
+                            in_=res[c][:, lo * TC:hi * TC].rearrange("p (i t) -> p i t", t=TC))
+
+        permute(0)
+        first_layer(0, 0)
+        first_layer(0, 1)
+        permute(1)
+        first_layer(1, 0)
+        first_layer(1, 1)
+        permute(2)
+        first_layer(2, 0)
+        first_layer(2, 1)
+        copy_z(0)
+        fir1(0)
+        copy_z(1)
+        fir1(1)
+        first_layer(0, 2)
+        first_layer(1, 2)
+        first_layer(2, 2)
+        first_layer(0, 3)
+        first_layer(1, 3)
+        first_layer(2, 3)
+        fir2(0)
+        fir2(1)
+        copy_z(2)
+        relu_s(0)
+        copy_z(3)
+        relu_s(1)
+        fir1(2)
+        quant(0)
+        second_layer(0)
+        fir1(3)
+        fir2(2)
+        quant(1)
+        second_layer(1)
+        bias_s(0, 0)
+        bias_s(0, 1)
+        store(0, 0, 4, nc.sync)
+        relu_s(2)
+        fir2(3)
+        quant(2)
+        second_layer(2)
+        relu_v(3)
+        bias_v(1, 1)
+        bias_s(1, 0)
+        store(1, 0, 4, nc.sync)
+        quant(3)
+        second_layer(3)
+        bias_v(2, 1)
+        bias_s(2, 0)
+        store(2, 0, 4, nc.sync)
+        bias_v(3, 1)
+        store(3, 2, 4, nc.sync)
+        bias_s(3, 0)
+        store(3, 0, 2, nc.scalar)

@@ -42,7 +42,8 @@ def tile_mix_momentum_of_two_inputs_kernel(
 
         wa_raw = sb.tile([P, 2 * 2 * R], U8, align_bytes=64)
         wc_raw = sb.tile([P, 2 * R], U8, align_bytes=64)
-        ws_raw = sb.tile([P, PASSES * R], U8, align_bytes=64)
+        was_raw = sb.tile([P, 2 * R], U8, align_bytes=64)
+        wcs_raw = sb.tile([P, R], U8, align_bytes=64)
         xts = sb.tile([P, 2 * T], U8, align_bytes=64)
         xqs = sb.tile([P, T], U8, align_bytes=64)
         wbs = sb.tile([P, N], U8, align_bytes=64)
@@ -55,24 +56,14 @@ def tile_mix_momentum_of_two_inputs_kernel(
         zs = sb.tile([P, PACK * (T + 1)], F32, align_bytes=64)
         ws = sb.tile([P, PACK * (T + 1)], F32, align_bytes=64)
         warm = sb.tile([P, 8], F32, align_bytes=64)
-
-        nc.vector.memset(ws_raw[:].bitcast(I32), 0)
-        nc.gpsimd.memset(xqs[:].bitcast(I32), 0)
-        nc.vector.memset(xts[:].bitcast(I32), 0)
-        nc.vector.memset(wbs[:].bitcast(I32), 0)
-        nc.vector.memset(zs[:, 0:PACK], 0.0)
-        nc.vector.memset(ws[:, 0:PACK], 0.0)
-        nc.vector.memset(warm[:], 0.0)
-
         ones = sb.tile([P, PACK * TC], BF16, align_bytes=64)
         ones_q = sb.tile([P, TC], I32, align_bytes=64)
         ones_s = sb.tile([P, TC], U8, align_bytes=64)
-        nc.vector.memset(ones[:], 1.0)
-        nc.vector.quantize_mx(out=ones_q[:].bitcast(FP8X4), scales=ones_s[:], in_=ones[:])
-        warm_bank = ps.tile([P, 2 * TC], F32, name="warm_bank", tag="y1_1")
-        for i in range(24):
-            nc.tensor.matmul_mx(out=warm_bank[:, (i % 2) * TC:(i % 2 + 1) * TC], lhsT=ones_q[:].bitcast(FP8X4), lhsT_scale=ones_s[:],
-                                rhs=ones_q[:].bitcast(FP8X4), rhs_scale=ones_s[:], start=True, stop=True)
+        xq_stage = sb.tile([P, T], I32, align_bytes=64)
+        wc_stage = sb.tile([P, T], I32, align_bytes=64)
+
+        def zero(eng, plane):
+            eng.memset(plane[:].bitcast(I32), 0)
 
         def load_words(queue, dst, src):
             z = src.shape[0]
@@ -82,37 +73,71 @@ def tile_mix_momentum_of_two_inputs_kernel(
         def fp8_rows(words):
             return words.rearrange("z p c t -> z p (c t)")
 
-        load_scale_rows(nc.gpsimd, xqs[:], xq_scales, range(4))
-        load_words(nc.sync, wa_raw[:], wa_words)
-        load_scale_rows(nc.scalar, ws_raw[:, 0:2 * R], wa_scales, range(4))
+        def stage_scales(queue, stage, scales):
+            queue.dma_start(out=stage[0:4, :].rearrange("r (q c) -> r q c", q=4),
+                            in_=scales.bitcast(I32)[0].rearrange("(q r) c -> r q c", r=4))
+
+        def spread_scales(eng, plane, stage):
+            for q in range(4):
+                eng.tensor_copy(out=plane[:].bitcast(I32)[32 * q:32 * q + 4, :], in_=stage[0:4, q * P:(q + 1) * P])
+
+        z_bank = [ps.tile([P, PACK * TC], F32, name="z_bank%d" % c) for c in range(CHUNKS)]
+        y_bank = [ps.tile([P, 2 * TC], F32, name="y_bank%d" % c) for c in range(4)]
+
+        def dummy(bank, n):
+            for i in range(n):
+                nc.tensor.matmul_mx(out=bank[:, (i % 2) * TC:(i % 2 + 1) * TC], lhsT=ones_q[:].bitcast(FP8X4), lhsT_scale=ones_s[:],
+                                    rhs=ones_q[:].bitcast(FP8X4), rhs_scale=ones_s[:], start=True, stop=True)
+
+        def keep_warm(n):
+            dummy(z_bank[0], n)
+
+        zero(nc.vector, was_raw)
+        zero(nc.vector, xts)
+        zero(nc.vector, xqs)
+        zero(nc.vector, wcs_raw)
+        nc.vector.memset(ones[:], 1.0)
+        nc.vector.quantize_mx(out=ones_q[:].bitcast(FP8X4), scales=ones_s[:], in_=ones[:])
+        dummy(y_bank[3], 24)
+        zero(nc.vector, wbs)
+        nc.vector.memset(zs[:, 0:PACK], 0.0)
+        nc.vector.memset(ws[:, 0:PACK], 0.0)
+        nc.vector.memset(warm[:], 0.0)
+        nc.scalar.activation(out=warm[:, 4:5], in_=warm[:, 0:1], func=ACT.Relu)
+
+        load_words(nc.gpsimd, xq[:], fp8_rows(xq_words))
+        load_scale_rows(nc.gpsimd, xqs[:], xq_scales, range(2))
         load_words(nc.sync, wc_raw[:], wc_words)
-        load_scale_rows(nc.scalar, ws_raw[:, 2 * R:3 * R], wc_scales, range(0, 2))
+        load_words(nc.sync, wa_raw[:], wa_words)
+        load_scale_rows(nc.sync, was_raw[:], wa_scales, range(4))
+        load_scale_rows(nc.sync, xts[:], xt_scales, range(0, 1))
         load_words(nc.sync, xt[:], fp8_rows(xt_words))
-        load_scale_rows(nc.scalar, ws_raw[:, 2 * R:3 * R], wc_scales, range(2, 4))
-        load_scale_rows(nc.scalar, xts[:], xt_scales, range(0, 2))
-        load_words(nc.sync, xq[:], fp8_rows(xq_words))
-        load_scale_rows(nc.sync, xts[:], xt_scales, range(2, 4))
+        load_scale_rows(nc.sync, xts[:], xt_scales, range(1, 4))
+        load_scale_rows(nc.sync, wcs_raw[:], wc_scales, range(4))
+        load_scale_rows(nc.sync, xqs[:], xq_scales, range(2, 4))
         load_words(nc.sync, wb[:], fp8_rows(wb_words))
         load_scale_rows(nc.sync, wbs[:], wb_scales, range(4))
         with nc.allow_non_contiguous_dma(reason="one bias value a partition"):
             nc.sync.dma_start(out=bias[:], in_=b.rearrange("(i p) o -> p (i o)", p=P))
 
-        nc.scalar.activation(out=warm[:, 4:5], in_=warm[:, 0:1], func=ACT.Relu)
-
         raw_words = [wa_raw[:, 0:2 * R], wa_raw[:, 2 * R:4 * R], wc_raw[:]]
+        raw_scales = [was_raw[:, 0:R], was_raw[:, R:2 * R], wcs_raw[:]]
         x_words = [xt[:, 0:T], xt[:, T:2 * T], xq[:]]
-
         x_scales = [xts[:, 0:T], xts[:, T:2 * T], xqs[:]]
 
-        def permute(g):
+        def permute_words(g):
             nc.vector.tensor_copy(
                 out=w_perm[g][:].bitcast(U16).rearrange("p (j m) -> p j m", j=PACK),
                 in_=raw_words[g].bitcast(U16).rearrange("p (m j) -> p j m", j=PACK))
+
+        def permute_scales(g):
             nc.vector.tensor_copy(
                 out=ws_perm[g][:].rearrange("p (j m) -> p j m", j=PACK),
-                in_=ws_raw[:, g * R:(g + 1) * R].rearrange("p (m j) -> p j m", j=PACK))
+                in_=raw_scales[g].rearrange("p (m j) -> p j m", j=PACK))
 
-        z_bank = [ps.tile([P, PACK * TC], F32, name="z_bank%d" % c) for c in range(CHUNKS)]
+        def permute(g):
+            permute_words(g)
+            permute_scales(g)
 
         def first_layer(g, c):
             for j in range(PACK):
@@ -126,121 +151,136 @@ def tile_mix_momentum_of_two_inputs_kernel(
                     stop=(g == PASSES - 1 and j == PACK - 1),
                 )
 
-        W = PACK * TC
-        h32 = [sb.tile([P, W], F32, align_bytes=64, name="h32_%d" % c) for c in range(CHUNKS)]
-        h16 = [sb.tile([P, W], BF16, align_bytes=64, name="h16_%d" % c) for c in range(CHUNKS)]
-        hq = [sb.tile([P, TC], I32, align_bytes=64, name="hq%d" % c) for c in range(CHUNKS)]
-        hs = [sb.tile([P, TC], U8, align_bytes=64, name="hs%d" % c) for c in range(CHUNKS)]
-        res = [sb.tile([P, W], F32, align_bytes=64, name="res%d" % c) for c in range(CHUNKS)]
-        y_bank = {}
+        h16 = sb.tile([P, PACK * T], BF16, align_bytes=64)
+        hr = sb.tile([P, PACK * T], BF16, align_bytes=64)
+        hq = sb.tile([P, T], I32, align_bytes=64)
+        hs = sb.tile([P, T], U8, align_bytes=64)
+        res = {}
+        banks = {}
 
-        def now(c):
-            return slice(PACK + c * W, PACK + (c + 1) * W)
+        def now(a, e):
+            return slice(PACK * (a + 1), PACK * (e + 1))
 
-        def before(c):
-            return slice(c * W, (c + 1) * W)
+        def flat(a, e):
+            return slice(PACK * a, PACK * e)
 
-        def copy_z(c):
-            nc.scalar.copy(out=zs[:, now(c)].rearrange("p (t j) -> p t j", j=PACK),
-                           in_=z_bank[c][:].rearrange("p (j t) -> p t j", j=PACK))
+        def copy(a, e):
+            c = a // TC
+            nc.scalar.copy(out=zs[:, now(a, e)].rearrange("p (t j) -> p t j", j=PACK),
+                           in_=z_bank[c][:].rearrange("p (j t) -> p t j", j=PACK)[:, a - c * TC:e - c * TC, :])
 
-        def fir1(c):
-            nc.vector.scalar_tensor_tensor(out=ws[:, now(c)], in0=zs[:, before(c)], scalar=0.5,
-                                           in1=zs[:, now(c)], op0=ALU.mult, op1=ALU.add)
+        def fir1(a, e):
+            nc.vector.scalar_tensor_tensor(out=ws[:, now(a, e)], in0=zs[:, flat(a, e)], scalar=0.5,
+                                           in1=zs[:, now(a, e)], op0=ALU.mult, op1=ALU.add)
 
-        def fir2(c):
-            nc.vector.scalar_tensor_tensor(out=h32[c][:], in0=ws[:, before(c)], scalar=0.5,
-                                           in1=zs[:, now(c)], op0=ALU.mult, op1=ALU.add)
+        def fir2(a, e):
+            nc.vector.scalar_tensor_tensor(out=h16[:, flat(a, e)], in0=ws[:, flat(a, e)], scalar=0.5,
+                                           in1=zs[:, now(a, e)], op0=ALU.mult, op1=ALU.add)
 
-        def relu_s(c):
-            nc.scalar.activation(out=h16[c][:], in_=h32[c][:], func=ACT.Relu)
+        def relu_s(a, e):
+            nc.scalar.activation(out=hr[:, flat(a, e)], in_=h16[:, flat(a, e)], func=ACT.Relu)
 
-        def relu_v(c):
-            nc.vector.tensor_scalar(out=h16[c][:], in0=h32[c][:], scalar1=0.0, scalar2=None, op0=ALU.max)
+        def relu_v(a, e):
+            nc.vector.tensor_scalar(out=hr[:, flat(a, e)], in0=h16[:, flat(a, e)], scalar1=0.0, scalar2=None, op0=ALU.max)
 
-        def quant(c):
-            nc.vector.quantize_mx(out=hq[c][:].bitcast(FP8X4), scales=hs[c][:], in_=h16[c][:])
+        def quant(a, e):
+            nc.vector.quantize_mx(out=hq[:, a:e].bitcast(FP8X4), scales=hs[:, a:e], in_=hr[:, flat(a, e)])
 
-        def second_layer(c):
+        def second(a, e):
+            w = e - a
+            k = len(res)
+            piece = sb.tile([P, PACK * w], F32, align_bytes=64, name="res%d" % a)
+            res[a] = piece
             for half in range(2):
-                bank = ps.tile([P, 2 * TC], F32, name="y%d_%d" % (c, half), tag="y%d_%d" % (c % 2, half))
-                y_bank[c, half] = bank
+                bank = (y_bank + z_bank[1:] + z_bank[0:1] + y_bank)[2 * k + half]
+                banks[a, half] = bank
                 for i in range(2):
                     n0 = (2 * half + i) * P
                     nc.tensor.matmul_mx(
-                        out=bank[:, i * TC:(i + 1) * TC],
+                        out=bank[:, i * w:(i + 1) * w],
                         lhsT=wb[:, n0:n0 + P].bitcast(FP8X4), lhsT_scale=wbs[:, n0:n0 + P],
-                        rhs=hq[c][:].bitcast(FP8X4), rhs_scale=hs[c][:],
+                        rhs=hq[:, a:e].bitcast(FP8X4), rhs_scale=hs[:, a:e],
                         start=True, stop=True)
 
-        def bias_s(c, half):
+        def bias_s(a, e, half):
+            w = e - a
             for i in range(2):
                 k = 2 * half + i
-                nc.scalar.activation(out=res[c][:, k * TC:(k + 1) * TC], in_=y_bank[c, half][:, i * TC:(i + 1) * TC],
+                nc.scalar.activation(out=res[a][:, k * w:(k + 1) * w], in_=banks[a, half][:, i * w:(i + 1) * w],
                                      func=ACT.Identity, bias=bias[:, k:k + 1])
 
-        def bias_v(c, half):
+        def bias_v(a, e, half):
+            w = e - a
             nc.vector.tensor_tensor(
-                out=res[c][:, 2 * half * TC:2 * (half + 1) * TC].rearrange("p (i t) -> p i t", i=2),
-                in0=y_bank[c, half][:].rearrange("p (i t) -> p i t", i=2),
-                in1=bias[:, 2 * half:2 * half + 2].unsqueeze(2).to_broadcast([P, 2, TC]),
+                out=res[a][:, 2 * half * w:2 * (half + 1) * w].rearrange("p (i t) -> p i t", i=2),
+                in0=banks[a, half][:, 0:2 * w].rearrange("p (i t) -> p i t", i=2),
+                in1=bias[:, 2 * half:2 * half + 2].unsqueeze(2).to_broadcast([P, 2, w]),
                 op=ALU.add)
 
         out_v = out.rearrange("(i p) t -> p i t", p=P)
 
-        def store(c, lo, hi, queue):
-            queue.dma_start(out=out_v[:, lo:hi, c * TC:(c + 1) * TC],
-                            in_=res[c][:, lo * TC:hi * TC].rearrange("p (i t) -> p i t", t=TC))
+        def store(a, e, lo, hi, queue):
+            w = e - a
+            queue.dma_start(out=out_v[:, lo:hi, a:e],
+                            in_=res[a][:, lo * w:hi * w].rearrange("p (i t) -> p i t", t=w))
 
+        permute_words(2)
         permute(0)
         first_layer(0, 0)
         first_layer(0, 1)
         permute(1)
         first_layer(1, 0)
         first_layer(1, 1)
-        permute(2)
+        permute_scales(2)
         first_layer(2, 0)
         first_layer(2, 1)
-        copy_z(0)
-        fir1(0)
-        copy_z(1)
-        fir1(1)
         first_layer(0, 2)
         first_layer(1, 2)
         first_layer(2, 2)
         first_layer(0, 3)
         first_layer(1, 3)
         first_layer(2, 3)
-        fir2(0)
-        fir2(1)
-        copy_z(2)
-        relu_s(0)
-        copy_z(3)
-        relu_s(1)
-        fir1(2)
-        quant(0)
-        second_layer(0)
-        fir1(3)
-        fir2(2)
-        quant(1)
-        second_layer(1)
-        bias_s(0, 0)
-        bias_s(0, 1)
-        store(0, 0, 4, nc.sync)
-        relu_s(2)
-        fir2(3)
-        quant(2)
-        second_layer(2)
-        relu_v(3)
-        bias_v(1, 1)
-        bias_s(1, 0)
-        store(1, 0, 4, nc.sync)
-        quant(3)
-        second_layer(3)
-        bias_v(2, 1)
-        bias_s(2, 0)
-        store(2, 0, 4, nc.sync)
-        bias_v(3, 1)
-        store(3, 2, 4, nc.sync)
-        bias_s(3, 0)
-        store(3, 0, 2, nc.scalar)
+
+        copy(0, 64)
+        copy(64, 128)
+        copy(128, 256)
+        keep_warm(12)
+        copy(256, 384)
+        fir1(0, 64)
+        fir1(64, 128)
+        fir2(0, 64)
+        fir2(64, 128)
+        relu_s(0, 128)
+        copy(384, 512)
+        fir1(128, 256)
+        fir1(256, 384)
+        fir2(128, 256)
+        relu_s(128, 256)
+        quant(0, 128)
+        second(0, 128)
+        keep_warm(6)
+        bias_s(0, 128, 0)
+        bias_s(0, 128, 1)
+        store(0, 128, 0, 4, nc.sync)
+        fir2(256, 384)
+        relu_s(256, 384)
+        fir1(384, 512)
+        quant(128, 256)
+        second(128, 256)
+        keep_warm(2)
+        bias_s(128, 256, 0)
+        bias_s(128, 256, 1)
+        store(128, 256, 0, 4, nc.sync)
+        fir2(384, 512)
+        quant(256, 384)
+        second(256, 384)
+        relu_v(384, 512)
+        quant(384, 512)
+        second(384, 512)
+        bias_s(256, 384, 0)
+        bias_v(256, 384, 1)
+        store(256, 384, 0, 4, nc.sync)
+        bias_v(384, 512, 0)
+        store(384, 512, 0, 2, nc.sync)
+        bias_s(384, 512, 1)
+        store(384, 512, 2, 4, nc.scalar)

@@ -17,17 +17,31 @@ ACT = mybir.ActivationFunctionType
 
 P = 128
 PACK = 4
-TC = 128
-CHUNKS = T // TC
-PASSES = 3
+QUADRANT = 32
+ROWS = 4
+CHUNK = 128
+CHUNKS = T // CHUNK
+PASSES = (K + L) // (P * PACK)
+PAIR = 2
+ALIGN = 64
+WARM_HEAD = 24
+WARM_PAUSES = (12, 6, 2)
 
 
-def load_scale_rows(queue, plane, scales, rows):
-    z = scales.shape[0]
-    src = scales.bitcast(I32).rearrange("z (q r) c -> r q z c", r=4)
-    dst = plane.bitcast(I32).rearrange("p (z c) -> p z c", z=z)
-    for r in rows:
-        queue.dma_start(out=dst[r:P:32], in_=src[r])
+def load_words(queue, tile, words):
+    passes = words.shape[0]
+    queue.dma_start(
+        out=tile[:].bitcast(I32).rearrange("p (g c) -> p g c", g=passes),
+        in_=words.bitcast(I32).rearrange("g p c -> p g c"),
+    )
+
+
+def load_scale_rows(queue, planes, scales, rows):
+    passes = scales.shape[0]
+    src = scales.bitcast(I32).rearrange("g (q i) c -> i q g c", i=ROWS)
+    dst = planes[:].bitcast(I32).rearrange("p (g c) -> p g c", g=passes)
+    for i in rows:
+        queue.dma_start(out=dst[i:P:QUADRANT], in_=src[i])
 
 
 def tile_mix_momentum_of_two_inputs_kernel(
@@ -40,247 +54,222 @@ def tile_mix_momentum_of_two_inputs_kernel(
         ps = ctx.enter_context(tc.psum_pool(name="ps", bufs=1))
         ctx.enter_context(tc.manual_schedule())
 
-        wa_raw = sb.tile([P, 2 * 2 * R], U8, align_bytes=64)
-        wc_raw = sb.tile([P, 2 * R], U8, align_bytes=64)
-        was_raw = sb.tile([P, 2 * R], U8, align_bytes=64)
-        wcs_raw = sb.tile([P, R], U8, align_bytes=64)
-        xts = sb.tile([P, 2 * T], U8, align_bytes=64)
-        xqs = sb.tile([P, T], U8, align_bytes=64)
-        wbs = sb.tile([P, N], U8, align_bytes=64)
-        xt = sb.tile([P, 2 * T], I32, align_bytes=64)
-        xq = sb.tile([P, T], I32, align_bytes=64)
-        wb = sb.tile([P, N], I32, align_bytes=64)
-        bias = sb.tile([P, N // P], F32, align_bytes=64)
-        w_perm = [sb.tile([P, 2 * R], U8, align_bytes=64, name="w_perm%d" % g) for g in range(PASSES)]
-        ws_perm = [sb.tile([P, R], U8, align_bytes=64, name="ws_perm%d" % g) for g in range(PASSES)]
-        zs = sb.tile([P, PACK * (T + 1)], F32, align_bytes=64)
-        ws = sb.tile([P, PACK * (T + 1)], F32, align_bytes=64)
-        warm = sb.tile([P, 8], F32, align_bytes=64)
-        ones = sb.tile([P, PACK * TC], BF16, align_bytes=64)
-        ones_q = sb.tile([P, TC], I32, align_bytes=64)
-        ones_s = sb.tile([P, TC], U8, align_bytes=64)
-        xq_stage = sb.tile([P, T], I32, align_bytes=64)
-        wc_stage = sb.tile([P, T], I32, align_bytes=64)
+        wa = sb.tile([P, 2 * 2 * R], U8, align_bytes=ALIGN)
+        wc = sb.tile([P, 2 * R], U8, align_bytes=ALIGN)
+        xt = sb.tile([P, 2 * T], I32, align_bytes=ALIGN)
+        xq = sb.tile([P, T], I32, align_bytes=ALIGN)
+        wb = sb.tile([P, N], I32, align_bytes=ALIGN)
+        wa_planes = sb.tile([P, 2 * R], U8, align_bytes=ALIGN)
+        wc_plane = sb.tile([P, R], U8, align_bytes=ALIGN)
+        xt_planes = sb.tile([P, 2 * T], U8, align_bytes=ALIGN)
+        xq_plane = sb.tile([P, T], U8, align_bytes=ALIGN)
+        wb_plane = sb.tile([P, N], U8, align_bytes=ALIGN)
+        bias = sb.tile([P, N // P], F32, align_bytes=ALIGN)
+        w_words = [sb.tile([P, 2 * R], U8, align_bytes=ALIGN, name="w_words%d" % g) for g in range(PASSES)]
+        w_plane = [sb.tile([P, R], U8, align_bytes=ALIGN, name="w_plane%d" % g) for g in range(PASSES)]
+        z = sb.tile([P, PACK * (T + 1)], F32, align_bytes=ALIGN)
+        u = sb.tile([P, PACK * (T + 1)], F32, align_bytes=ALIGN)
+        pre = sb.tile([P, PACK * T], BF16, align_bytes=ALIGN)
+        hid = sb.tile([P, PACK * T], BF16, align_bytes=ALIGN)
+        hid_words = sb.tile([P, T], I32, align_bytes=ALIGN)
+        hid_plane = sb.tile([P, T], U8, align_bytes=ALIGN)
+        result = [sb.tile([P, N // P * CHUNK], F32, align_bytes=ALIGN, name="result%d" % c) for c in range(CHUNKS)]
 
-        def zero(eng, plane):
-            eng.memset(plane[:].bitcast(I32), 0)
+        z_bank = [ps.tile([P, PACK * CHUNK], F32, name="z_bank%d" % c) for c in range(CHUNKS)]
+        spare_bank = [ps.tile([P, PAIR * CHUNK], F32, name="spare_bank%d" % i) for i in range(4)]
+        p_bank = spare_bank + z_bank[1:] + z_bank[:1]
 
-        def load_words(queue, dst, src):
-            z = src.shape[0]
-            queue.dma_start(out=dst.bitcast(I32).rearrange("p (z c) -> p z c", z=z),
-                            in_=src.bitcast(I32).rearrange("z p c -> p z c"))
+        nc.gpsimd.memset(xq_plane[:].bitcast(I32), 0)
+        for plane in (wa_planes, xt_planes, wc_plane):
+            nc.vector.memset(plane[:].bitcast(I32), 0)
 
-        def fp8_rows(words):
-            return words.rearrange("z p c t -> z p (c t)")
-
-        def stage_scales(queue, stage, scales):
-            queue.dma_start(out=stage[0:4, :].rearrange("r (q c) -> r q c", q=4),
-                            in_=scales.bitcast(I32)[0].rearrange("(q r) c -> r q c", r=4))
-
-        def spread_scales(eng, plane, stage):
-            for q in range(4):
-                eng.tensor_copy(out=plane[:].bitcast(I32)[32 * q:32 * q + 4, :], in_=stage[0:4, q * P:(q + 1) * P])
-
-        z_bank = [ps.tile([P, PACK * TC], F32, name="z_bank%d" % c) for c in range(CHUNKS)]
-        y_bank = [ps.tile([P, 2 * TC], F32, name="y_bank%d" % c) for c in range(4)]
-
-        def dummy(bank, n):
-            for i in range(n):
-                nc.tensor.matmul_mx(out=bank[:, (i % 2) * TC:(i % 2 + 1) * TC], lhsT=ones_q[:].bitcast(FP8X4), lhsT_scale=ones_s[:],
-                                    rhs=ones_q[:].bitcast(FP8X4), rhs_scale=ones_s[:], start=True, stop=True)
-
-        def keep_warm(n):
-            dummy(z_bank[0], n)
-
-        zero(nc.vector, was_raw)
-        zero(nc.vector, xts)
-        zero(nc.vector, xqs)
-        zero(nc.vector, wcs_raw)
+        ones = sb.tile([P, PACK * CHUNK], BF16, align_bytes=ALIGN)
+        ones_words = sb.tile([P, CHUNK], I32, align_bytes=ALIGN)
+        ones_plane = sb.tile([P, CHUNK], U8, align_bytes=ALIGN)
         nc.vector.memset(ones[:], 1.0)
-        nc.vector.quantize_mx(out=ones_q[:].bitcast(FP8X4), scales=ones_s[:], in_=ones[:])
-        dummy(y_bank[3], 24)
-        zero(nc.vector, wbs)
-        nc.vector.memset(zs[:, 0:PACK], 0.0)
-        nc.vector.memset(ws[:, 0:PACK], 0.0)
-        nc.vector.memset(warm[:], 0.0)
-        nc.scalar.activation(out=warm[:, 4:5], in_=warm[:, 0:1], func=ACT.Relu)
+        nc.vector.quantize_mx(out=ones_words[:].bitcast(FP8X4), scales=ones_plane[:], in_=ones[:])
 
-        load_words(nc.gpsimd, xq[:], fp8_rows(xq_words))
-        load_scale_rows(nc.gpsimd, xqs[:], xq_scales, range(2))
-        load_words(nc.sync, wc_raw[:], wc_words)
-        load_words(nc.sync, wa_raw[:], wa_words)
-        load_scale_rows(nc.sync, was_raw[:], wa_scales, range(4))
-        load_scale_rows(nc.sync, xts[:], xt_scales, range(0, 1))
-        load_words(nc.sync, xt[:], fp8_rows(xt_words))
-        load_scale_rows(nc.sync, xts[:], xt_scales, range(1, 4))
-        load_scale_rows(nc.sync, wcs_raw[:], wc_scales, range(4))
-        load_scale_rows(nc.sync, xqs[:], xq_scales, range(2, 4))
-        load_words(nc.sync, wb[:], fp8_rows(wb_words))
-        load_scale_rows(nc.sync, wbs[:], wb_scales, range(4))
-        with nc.allow_non_contiguous_dma(reason="one bias value a partition"):
+        def warm_tensor(bank, count):
+            for i in range(count):
+                nc.tensor.matmul_mx(
+                    out=bank[:, (i % PAIR) * CHUNK:(i % PAIR + 1) * CHUNK],
+                    lhsT=ones_words[:].bitcast(FP8X4), lhsT_scale=ones_plane[:],
+                    rhs=ones_words[:].bitcast(FP8X4), rhs_scale=ones_plane[:],
+                    start=True, stop=True,
+                )
+
+        warm_tensor(spare_bank[-1], WARM_HEAD)
+
+        nc.vector.memset(wb_plane[:].bitcast(I32), 0)
+        nc.vector.memset(u[:, 0:PACK], 0.0)
+        nc.scalar.activation(out=z[:, 0:PACK], in_=u[:, 0:PACK], func=ACT.Relu)
+
+        load_scale_rows(nc.gpsimd, xq_plane, xq_scales, range(0, 2))
+        load_words(nc.sync, wc, wc_words)
+        load_words(nc.sync, wa, wa_words)
+        load_scale_rows(nc.sync, wa_planes, wa_scales, range(ROWS))
+        load_scale_rows(nc.sync, xt_planes, xt_scales, range(0, 1))
+        load_words(nc.sync, xt, xt_words.rearrange("g p c j -> g p (c j)"))
+        load_scale_rows(nc.sync, xt_planes, xt_scales, range(1, ROWS))
+        load_scale_rows(nc.sync, wc_plane, wc_scales, range(ROWS))
+        load_words(nc.sync, xq, xq_words.rearrange("g p c j -> g p (c j)"))
+        load_scale_rows(nc.sync, xq_plane, xq_scales, range(2, ROWS))
+        load_words(nc.sync, wb, wb_words.rearrange("g p c j -> g p (c j)"))
+        load_scale_rows(nc.sync, wb_plane, wb_scales, range(ROWS))
+        with nc.allow_non_contiguous_dma(reason="bias[p, i] = b[128 i + p]: one value a partition and tile"):
             nc.sync.dma_start(out=bias[:], in_=b.rearrange("(i p) o -> p (i o)", p=P))
 
-        raw_words = [wa_raw[:, 0:2 * R], wa_raw[:, 2 * R:4 * R], wc_raw[:]]
-        raw_scales = [was_raw[:, 0:R], was_raw[:, R:2 * R], wcs_raw[:]]
+        raw_words = [wa[:, 0:2 * R], wa[:, 2 * R:4 * R], wc[:]]
+        raw_plane = [wa_planes[:, 0:R], wa_planes[:, R:2 * R], wc_plane[:]]
         x_words = [xt[:, 0:T], xt[:, T:2 * T], xq[:]]
-        x_scales = [xts[:, 0:T], xts[:, T:2 * T], xqs[:]]
+        x_plane = [xt_planes[:, 0:T], xt_planes[:, T:2 * T], xq_plane[:]]
 
-        def permute_words(g):
+        def reorder_words(g):
             nc.vector.tensor_copy(
-                out=w_perm[g][:].bitcast(U16).rearrange("p (j m) -> p j m", j=PACK),
-                in_=raw_words[g].bitcast(U16).rearrange("p (m j) -> p j m", j=PACK))
+                out=w_words[g][:].bitcast(U16).rearrange("k (j p) -> k j p", j=PACK),
+                in_=raw_words[g].bitcast(U16).rearrange("k (p j) -> k j p", j=PACK),
+            )
 
-        def permute_scales(g):
+        def reorder_scales(g):
             nc.vector.tensor_copy(
-                out=ws_perm[g][:].rearrange("p (j m) -> p j m", j=PACK),
-                in_=raw_scales[g].rearrange("p (m j) -> p j m", j=PACK))
-
-        def permute(g):
-            permute_words(g)
-            permute_scales(g)
+                out=w_plane[g][:].rearrange("k (j p) -> k j p", j=PACK),
+                in_=raw_plane[g].rearrange("k (p j) -> k j p", j=PACK),
+            )
 
         def first_layer(g, c):
+            tokens = slice(c * CHUNK, (c + 1) * CHUNK)
             for j in range(PACK):
                 nc.tensor.matmul_mx(
-                    out=z_bank[c][:, j * TC:(j + 1) * TC],
-                    lhsT=w_perm[g][:, 2 * P * j:2 * P * (j + 1)].bitcast(FP4X4),
-                    lhsT_scale=ws_perm[g][:, P * j:P * (j + 1)],
-                    rhs=x_words[g][:, c * TC:(c + 1) * TC].bitcast(FP8X4),
-                    rhs_scale=x_scales[g][:, c * TC:(c + 1) * TC],
+                    out=z_bank[c][:, j * CHUNK:(j + 1) * CHUNK],
+                    lhsT=w_words[g][:, 2 * P * j:2 * P * (j + 1)].bitcast(FP4X4),
+                    lhsT_scale=w_plane[g][:, P * j:P * (j + 1)],
+                    rhs=x_words[g][:, tokens].bitcast(FP8X4),
+                    rhs_scale=x_plane[g][:, tokens],
                     start=(g == 0 and j == 0),
                     stop=(g == PASSES - 1 and j == PACK - 1),
                 )
 
-        h16 = sb.tile([P, PACK * T], BF16, align_bytes=64)
-        hr = sb.tile([P, PACK * T], BF16, align_bytes=64)
-        hq = sb.tile([P, T], I32, align_bytes=64)
-        hs = sb.tile([P, T], U8, align_bytes=64)
-        res = {}
-        banks = {}
+        def columns(tokens):
+            return slice(PACK * tokens[0], PACK * tokens[1])
 
-        def now(a, e):
-            return slice(PACK * (a + 1), PACK * (e + 1))
+        def padded(tokens):
+            return slice(PACK * (tokens[0] + 1), PACK * (tokens[1] + 1))
 
-        def flat(a, e):
-            return slice(PACK * a, PACK * e)
+        def copy_z(tokens):
+            c = tokens[0] // CHUNK
+            by_token = z_bank[c][:].rearrange("p (j t) -> p t j", j=PACK)
+            nc.scalar.copy(
+                out=z[:, padded(tokens)].rearrange("p (t j) -> p t j", j=PACK),
+                in_=by_token[:, tokens[0] - c * CHUNK:tokens[1] - c * CHUNK, :],
+            )
 
-        def copy(a, e):
-            c = a // TC
-            nc.scalar.copy(out=zs[:, now(a, e)].rearrange("p (t j) -> p t j", j=PACK),
-                           in_=z_bank[c][:].rearrange("p (j t) -> p t j", j=PACK)[:, a - c * TC:e - c * TC, :])
+        def make_u(tokens):
+            nc.vector.scalar_tensor_tensor(
+                out=u[:, padded(tokens)], in0=z[:, columns(tokens)], scalar=0.5,
+                in1=z[:, padded(tokens)], op0=ALU.mult, op1=ALU.add,
+            )
 
-        def fir1(a, e):
-            nc.vector.scalar_tensor_tensor(out=ws[:, now(a, e)], in0=zs[:, flat(a, e)], scalar=0.5,
-                                           in1=zs[:, now(a, e)], op0=ALU.mult, op1=ALU.add)
+        def make_pre(tokens):
+            nc.vector.scalar_tensor_tensor(
+                out=pre[:, columns(tokens)], in0=u[:, columns(tokens)], scalar=0.5,
+                in1=z[:, padded(tokens)], op0=ALU.mult, op1=ALU.add,
+            )
 
-        def fir2(a, e):
-            nc.vector.scalar_tensor_tensor(out=h16[:, flat(a, e)], in0=ws[:, flat(a, e)], scalar=0.5,
-                                           in1=zs[:, now(a, e)], op0=ALU.mult, op1=ALU.add)
+        def relu_on_scalar(tokens):
+            nc.scalar.activation(out=hid[:, columns(tokens)], in_=pre[:, columns(tokens)], func=ACT.Relu)
 
-        def relu_s(a, e):
-            nc.scalar.activation(out=hr[:, flat(a, e)], in_=h16[:, flat(a, e)], func=ACT.Relu)
+        def relu_on_vector(tokens):
+            nc.vector.tensor_scalar(
+                out=hid[:, columns(tokens)], in0=pre[:, columns(tokens)], scalar1=0.0, scalar2=None, op0=ALU.max,
+            )
 
-        def relu_v(a, e):
-            nc.vector.tensor_scalar(out=hr[:, flat(a, e)], in0=h16[:, flat(a, e)], scalar1=0.0, scalar2=None, op0=ALU.max)
+        def second_layer(c):
+            tokens = slice(c * CHUNK, (c + 1) * CHUNK)
+            nc.vector.quantize_mx(
+                out=hid_words[:, tokens].bitcast(FP8X4), scales=hid_plane[:, tokens], in_=hid[:, columns(chunk[c])],
+            )
+            for i in range(N // P):
+                rows = slice(i * P, (i + 1) * P)
+                nc.tensor.matmul_mx(
+                    out=p_bank[PAIR * c + i // PAIR][:, (i % PAIR) * CHUNK:(i % PAIR + 1) * CHUNK],
+                    lhsT=wb[:, rows].bitcast(FP8X4), lhsT_scale=wb_plane[:, rows],
+                    rhs=hid_words[:, tokens].bitcast(FP8X4), rhs_scale=hid_plane[:, tokens],
+                    start=True, stop=True,
+                )
 
-        def quant(a, e):
-            nc.vector.quantize_mx(out=hq[:, a:e].bitcast(FP8X4), scales=hs[:, a:e], in_=hr[:, flat(a, e)])
+        def bias_on_scalar(c, half):
+            for i in range(PAIR * half, PAIR * (half + 1)):
+                nc.scalar.activation(
+                    out=result[c][:, i * CHUNK:(i + 1) * CHUNK],
+                    in_=p_bank[PAIR * c + half][:, (i % PAIR) * CHUNK:(i % PAIR + 1) * CHUNK],
+                    func=ACT.Identity, bias=bias[:, i:i + 1],
+                )
 
-        def second(a, e):
-            w = e - a
-            k = len(res)
-            piece = sb.tile([P, PACK * w], F32, align_bytes=64, name="res%d" % a)
-            res[a] = piece
-            for half in range(2):
-                bank = (y_bank + z_bank[1:] + z_bank[0:1] + y_bank)[2 * k + half]
-                banks[a, half] = bank
-                for i in range(2):
-                    n0 = (2 * half + i) * P
-                    nc.tensor.matmul_mx(
-                        out=bank[:, i * w:(i + 1) * w],
-                        lhsT=wb[:, n0:n0 + P].bitcast(FP8X4), lhsT_scale=wbs[:, n0:n0 + P],
-                        rhs=hq[:, a:e].bitcast(FP8X4), rhs_scale=hs[:, a:e],
-                        start=True, stop=True)
-
-        def bias_s(a, e, half):
-            w = e - a
-            for i in range(2):
-                k = 2 * half + i
-                nc.scalar.activation(out=res[a][:, k * w:(k + 1) * w], in_=banks[a, half][:, i * w:(i + 1) * w],
-                                     func=ACT.Identity, bias=bias[:, k:k + 1])
-
-        def bias_v(a, e, half):
-            w = e - a
+        def bias_on_vector(c, half):
+            tiles = slice(PAIR * half, PAIR * (half + 1))
             nc.vector.tensor_tensor(
-                out=res[a][:, 2 * half * w:2 * (half + 1) * w].rearrange("p (i t) -> p i t", i=2),
-                in0=banks[a, half][:, 0:2 * w].rearrange("p (i t) -> p i t", i=2),
-                in1=bias[:, 2 * half:2 * half + 2].unsqueeze(2).to_broadcast([P, 2, w]),
-                op=ALU.add)
+                out=result[c][:].rearrange("p (i t) -> p i t", t=CHUNK)[:, tiles, :],
+                in0=p_bank[PAIR * c + half][:, 0:PAIR * CHUNK].rearrange("p (i t) -> p i t", t=CHUNK),
+                in1=bias[:, tiles].unsqueeze(2).to_broadcast([P, PAIR, CHUNK]),
+                op=ALU.add,
+            )
 
-        out_v = out.rearrange("(i p) t -> p i t", p=P)
+        out_tiles = out.rearrange("(i p) t -> p i t", p=P)
 
-        def store(a, e, lo, hi, queue):
-            w = e - a
-            queue.dma_start(out=out_v[:, lo:hi, a:e],
-                            in_=res[a][:, lo * w:hi * w].rearrange("p (i t) -> p i t", t=w))
+        def store(queue, c, tiles):
+            queue.dma_start(
+                out=out_tiles[:, tiles, c * CHUNK:(c + 1) * CHUNK],
+                in_=result[c][:].rearrange("p (i t) -> p i t", t=CHUNK)[:, tiles, :],
+            )
 
-        permute_words(2)
-        permute(0)
-        first_layer(0, 0)
-        first_layer(0, 1)
-        permute(1)
-        first_layer(1, 0)
-        first_layer(1, 1)
-        permute_scales(2)
-        first_layer(2, 0)
-        first_layer(2, 1)
-        first_layer(0, 2)
-        first_layer(1, 2)
-        first_layer(2, 2)
-        first_layer(0, 3)
-        first_layer(1, 3)
-        first_layer(2, 3)
+        chunk = [(c * CHUNK, (c + 1) * CHUNK) for c in range(CHUNKS)]
+        first_halves = [(0, CHUNK // 2), (CHUNK // 2, CHUNK)]
+        all_tiles = slice(0, N // P)
 
-        copy(0, 64)
-        copy(64, 128)
-        copy(128, 256)
-        keep_warm(12)
-        copy(256, 384)
-        fir1(0, 64)
-        fir1(64, 128)
-        fir2(0, 64)
-        fir2(64, 128)
-        relu_s(0, 128)
-        copy(384, 512)
-        fir1(128, 256)
-        fir1(256, 384)
-        fir2(128, 256)
-        relu_s(128, 256)
-        quant(0, 128)
-        second(0, 128)
-        keep_warm(6)
-        bias_s(0, 128, 0)
-        bias_s(0, 128, 1)
-        store(0, 128, 0, 4, nc.sync)
-        fir2(256, 384)
-        relu_s(256, 384)
-        fir1(384, 512)
-        quant(128, 256)
-        second(128, 256)
-        keep_warm(2)
-        bias_s(128, 256, 0)
-        bias_s(128, 256, 1)
-        store(128, 256, 0, 4, nc.sync)
-        fir2(384, 512)
-        quant(256, 384)
-        second(256, 384)
-        relu_v(384, 512)
-        quant(384, 512)
-        second(384, 512)
-        bias_s(256, 384, 0)
-        bias_v(256, 384, 1)
-        store(256, 384, 0, 4, nc.sync)
-        bias_v(384, 512, 0)
-        store(384, 512, 0, 2, nc.sync)
-        bias_s(384, 512, 1)
-        store(384, 512, 2, 4, nc.scalar)
+        reorder_words(2)
+        for g in range(PASSES):
+            if g < 2:
+                reorder_words(g)
+            reorder_scales(g)
+            first_layer(g, 0)
+            first_layer(g, 1)
+        for c in range(2, CHUNKS):
+            for g in range(PASSES):
+                first_layer(g, c)
+
+        for tokens in first_halves:
+            copy_z(tokens)
+        copy_z(chunk[1])
+        warm_tensor(z_bank[0], WARM_PAUSES[0])
+        copy_z(chunk[2])
+        for tokens in first_halves:
+            make_u(tokens)
+        for tokens in first_halves:
+            make_pre(tokens)
+        relu_on_scalar(chunk[0])
+        copy_z(chunk[3])
+        make_u(chunk[1])
+        make_u(chunk[2])
+
+        for c in range(2):
+            make_pre(chunk[c + 1])
+            relu_on_scalar(chunk[c + 1])
+            if c == 1:
+                make_u(chunk[3])
+            second_layer(c)
+            warm_tensor(z_bank[0], WARM_PAUSES[c + 1])
+            bias_on_scalar(c, 0)
+            bias_on_scalar(c, 1)
+            store(nc.sync, c, all_tiles)
+
+        make_pre(chunk[3])
+        second_layer(2)
+        relu_on_vector(chunk[3])
+        second_layer(3)
+        bias_on_scalar(2, 0)
+        bias_on_vector(2, 1)
+        store(nc.sync, 2, all_tiles)
+        bias_on_vector(3, 0)
+        store(nc.sync, 3, slice(0, PAIR))
+        bias_on_scalar(3, 1)
+        store(nc.scalar, 3, slice(PAIR, N // P))

from contextlib import ExitStack

import concourse.mybir as mybir

K, L, T, R, N = 1024, 512, 512, 512, 512
FLOPS = 2 * (K + L) * R * T + 2 * R * N * T

F32 = mybir.dt.float32
BF16 = mybir.dt.bfloat16
I32 = mybir.dt.int32
U16 = mybir.dt.uint16
U8 = mybir.dt.uint8
FP8X4 = mybir.dt.float8_e4m3fn_x4
FP4X4 = mybir.dt.float4_e2m1fn_x4
ALU = mybir.AluOpType
ACT = mybir.ActivationFunctionType

P = 128
PACK = 4
QUADRANT = 32
ROWS = 4
CHUNK = 128
CHUNKS = T // CHUNK
PASSES = (K + L) // (P * PACK)
PAIR = 2
ALIGN = 64
WARM_HEAD = 24
WARM_PAUSES = (12, 6, 2)


def load_words(queue, tile, words):
    passes = words.shape[0]
    queue.dma_start(
        out=tile[:].bitcast(I32).rearrange("p (g c) -> p g c", g=passes),
        in_=words.bitcast(I32).rearrange("g p c -> p g c"),
    )


def load_scale_rows(queue, planes, scales, rows):
    passes = scales.shape[0]
    src = scales.bitcast(I32).rearrange("g (q i) c -> i q g c", i=ROWS)
    dst = planes[:].bitcast(I32).rearrange("p (g c) -> p g c", g=passes)
    for i in rows:
        queue.dma_start(out=dst[i:P:QUADRANT], in_=src[i])


def tile_mix_momentum_of_two_inputs_kernel(
    tc, xt_words, xt_scales, wa_words, wa_scales, xq_words, xq_scales,
    wc_words, wc_scales, wb_words, wb_scales, b, out,
):
    nc = tc.nc
    with ExitStack() as ctx:
        sb = ctx.enter_context(tc.tile_pool(name="sb", bufs=1))
        ps = ctx.enter_context(tc.psum_pool(name="ps", bufs=1))
        ctx.enter_context(tc.manual_schedule())

        wa = sb.tile([P, 2 * 2 * R], U8, align_bytes=ALIGN)
        wc = sb.tile([P, 2 * R], U8, align_bytes=ALIGN)
        xt = sb.tile([P, 2 * T], I32, align_bytes=ALIGN)
        xq = sb.tile([P, T], I32, align_bytes=ALIGN)
        wb = sb.tile([P, N], I32, align_bytes=ALIGN)
        wa_planes = sb.tile([P, 2 * R], U8, align_bytes=ALIGN)
        wc_plane = sb.tile([P, R], U8, align_bytes=ALIGN)
        xt_planes = sb.tile([P, 2 * T], U8, align_bytes=ALIGN)
        xq_plane = sb.tile([P, T], U8, align_bytes=ALIGN)
        wb_plane = sb.tile([P, N], U8, align_bytes=ALIGN)
        bias = sb.tile([P, N // P], F32, align_bytes=ALIGN)
        w_words = [sb.tile([P, 2 * R], U8, align_bytes=ALIGN, name="w_words%d" % g) for g in range(PASSES)]
        w_plane = [sb.tile([P, R], U8, align_bytes=ALIGN, name="w_plane%d" % g) for g in range(PASSES)]
        z = sb.tile([P, PACK * (T + 1)], F32, align_bytes=ALIGN)
        u = sb.tile([P, PACK * (T + 1)], F32, align_bytes=ALIGN)
        pre = sb.tile([P, PACK * T], BF16, align_bytes=ALIGN)
        hid = sb.tile([P, PACK * T], BF16, align_bytes=ALIGN)
        hid_words = sb.tile([P, T], I32, align_bytes=ALIGN)
        hid_plane = sb.tile([P, T], U8, align_bytes=ALIGN)
        result = [sb.tile([P, N // P * CHUNK], F32, align_bytes=ALIGN, name="result%d" % c) for c in range(CHUNKS)]

        z_bank = [ps.tile([P, PACK * CHUNK], F32, name="z_bank%d" % c) for c in range(CHUNKS)]
        spare_bank = [ps.tile([P, PAIR * CHUNK], F32, name="spare_bank%d" % i) for i in range(4)]
        p_bank = spare_bank + z_bank[1:] + z_bank[:1]

        nc.gpsimd.memset(xq_plane[:].bitcast(I32), 0)
        for plane in (wa_planes, xt_planes, wc_plane):
            nc.vector.memset(plane[:].bitcast(I32), 0)

        ones = sb.tile([P, PACK * CHUNK], BF16, align_bytes=ALIGN)
        ones_words = sb.tile([P, CHUNK], I32, align_bytes=ALIGN)
        ones_plane = sb.tile([P, CHUNK], U8, align_bytes=ALIGN)
        nc.vector.memset(ones[:], 1.0)
        nc.vector.quantize_mx(out=ones_words[:].bitcast(FP8X4), scales=ones_plane[:], in_=ones[:])

        def warm_tensor(bank, count):
            for i in range(count):
                nc.tensor.matmul_mx(
                    out=bank[:, (i % PAIR) * CHUNK:(i % PAIR + 1) * CHUNK],
                    lhsT=ones_words[:].bitcast(FP8X4), lhsT_scale=ones_plane[:],
                    rhs=ones_words[:].bitcast(FP8X4), rhs_scale=ones_plane[:],
                    start=True, stop=True,
                )

        warm_tensor(spare_bank[-1], WARM_HEAD)

        nc.vector.memset(wb_plane[:].bitcast(I32), 0)
        nc.vector.memset(u[:, 0:PACK], 0.0)
        nc.scalar.activation(out=z[:, 0:PACK], in_=u[:, 0:PACK], func=ACT.Relu)

        load_scale_rows(nc.gpsimd, xq_plane, xq_scales, range(0, 2))
        load_words(nc.sync, wc, wc_words)
        load_words(nc.sync, wa, wa_words)
        load_scale_rows(nc.sync, wa_planes, wa_scales, range(ROWS))
        load_scale_rows(nc.sync, xt_planes, xt_scales, range(0, 1))
        load_words(nc.sync, xt, xt_words.rearrange("g p c j -> g p (c j)"))
        load_scale_rows(nc.sync, xt_planes, xt_scales, range(1, ROWS))
        load_scale_rows(nc.sync, wc_plane, wc_scales, range(ROWS))
        load_words(nc.sync, xq, xq_words.rearrange("g p c j -> g p (c j)"))
        load_scale_rows(nc.sync, xq_plane, xq_scales, range(2, ROWS))
        load_words(nc.sync, wb, wb_words.rearrange("g p c j -> g p (c j)"))
        load_scale_rows(nc.sync, wb_plane, wb_scales, range(ROWS))
        with nc.allow_non_contiguous_dma(reason="bias[p, i] = b[128 i + p]: one value a partition and tile"):
            nc.sync.dma_start(out=bias[:], in_=b.rearrange("(i p) o -> p (i o)", p=P))

        raw_words = [wa[:, 0:2 * R], wa[:, 2 * R:4 * R], wc[:]]
        raw_plane = [wa_planes[:, 0:R], wa_planes[:, R:2 * R], wc_plane[:]]
        x_words = [xt[:, 0:T], xt[:, T:2 * T], xq[:]]
        x_plane = [xt_planes[:, 0:T], xt_planes[:, T:2 * T], xq_plane[:]]

        def reorder_words(g):
            nc.vector.tensor_copy(
                out=w_words[g][:].bitcast(U16).rearrange("k (j p) -> k j p", j=PACK),
                in_=raw_words[g].bitcast(U16).rearrange("k (p j) -> k j p", j=PACK),
            )

        def reorder_scales(g):
            nc.vector.tensor_copy(
                out=w_plane[g][:].rearrange("k (j p) -> k j p", j=PACK),
                in_=raw_plane[g].rearrange("k (p j) -> k j p", j=PACK),
            )

        def first_layer(g, c):
            tokens = slice(c * CHUNK, (c + 1) * CHUNK)
            for j in range(PACK):
                nc.tensor.matmul_mx(
                    out=z_bank[c][:, j * CHUNK:(j + 1) * CHUNK],
                    lhsT=w_words[g][:, 2 * P * j:2 * P * (j + 1)].bitcast(FP4X4),
                    lhsT_scale=w_plane[g][:, P * j:P * (j + 1)],
                    rhs=x_words[g][:, tokens].bitcast(FP8X4),
                    rhs_scale=x_plane[g][:, tokens],
                    start=(g == 0 and j == 0),
                    stop=(g == PASSES - 1 and j == PACK - 1),
                )

        def columns(tokens):
            return slice(PACK * tokens[0], PACK * tokens[1])

        def padded(tokens):
            return slice(PACK * (tokens[0] + 1), PACK * (tokens[1] + 1))

        def copy_z(tokens):
            c = tokens[0] // CHUNK
            by_token = z_bank[c][:].rearrange("p (j t) -> p t j", j=PACK)
            nc.scalar.copy(
                out=z[:, padded(tokens)].rearrange("p (t j) -> p t j", j=PACK),
                in_=by_token[:, tokens[0] - c * CHUNK:tokens[1] - c * CHUNK, :],
            )

        def make_u(tokens):
            nc.vector.scalar_tensor_tensor(
                out=u[:, padded(tokens)], in0=z[:, columns(tokens)], scalar=0.5,
                in1=z[:, padded(tokens)], op0=ALU.mult, op1=ALU.add,
            )

        def make_pre(tokens):
            nc.vector.scalar_tensor_tensor(
                out=pre[:, columns(tokens)], in0=u[:, columns(tokens)], scalar=0.5,
                in1=z[:, padded(tokens)], op0=ALU.mult, op1=ALU.add,
            )

        def relu_on_scalar(tokens):
            nc.scalar.activation(out=hid[:, columns(tokens)], in_=pre[:, columns(tokens)], func=ACT.Relu)

        def relu_on_vector(tokens):
            nc.vector.tensor_scalar(
                out=hid[:, columns(tokens)], in0=pre[:, columns(tokens)], scalar1=0.0, scalar2=None, op0=ALU.max,
            )

        def second_layer(c):
            tokens = slice(c * CHUNK, (c + 1) * CHUNK)
            nc.vector.quantize_mx(
                out=hid_words[:, tokens].bitcast(FP8X4), scales=hid_plane[:, tokens], in_=hid[:, columns(chunk[c])],
            )
            for i in range(N // P):
                rows = slice(i * P, (i + 1) * P)
                nc.tensor.matmul_mx(
                    out=p_bank[PAIR * c + i // PAIR][:, (i % PAIR) * CHUNK:(i % PAIR + 1) * CHUNK],
                    lhsT=wb[:, rows].bitcast(FP8X4), lhsT_scale=wb_plane[:, rows],
                    rhs=hid_words[:, tokens].bitcast(FP8X4), rhs_scale=hid_plane[:, tokens],
                    start=True, stop=True,
                )

        def bias_on_scalar(c, half):
            for i in range(PAIR * half, PAIR * (half + 1)):
                nc.scalar.activation(
                    out=result[c][:, i * CHUNK:(i + 1) * CHUNK],
                    in_=p_bank[PAIR * c + half][:, (i % PAIR) * CHUNK:(i % PAIR + 1) * CHUNK],
                    func=ACT.Identity, bias=bias[:, i:i + 1],
                )

        def bias_on_vector(c, half):
            tiles = slice(PAIR * half, PAIR * (half + 1))
            nc.vector.tensor_tensor(
                out=result[c][:].rearrange("p (i t) -> p i t", t=CHUNK)[:, tiles, :],
                in0=p_bank[PAIR * c + half][:, 0:PAIR * CHUNK].rearrange("p (i t) -> p i t", t=CHUNK),
                in1=bias[:, tiles].unsqueeze(2).to_broadcast([P, PAIR, CHUNK]),
                op=ALU.add,
            )

        out_tiles = out.rearrange("(i p) t -> p i t", p=P)

        def store(queue, c, tiles):
            queue.dma_start(
                out=out_tiles[:, tiles, c * CHUNK:(c + 1) * CHUNK],
                in_=result[c][:].rearrange("p (i t) -> p i t", t=CHUNK)[:, tiles, :],
            )

        chunk = [(c * CHUNK, (c + 1) * CHUNK) for c in range(CHUNKS)]
        first_halves = [(0, CHUNK // 2), (CHUNK // 2, CHUNK)]
        all_tiles = slice(0, N // P)

        reorder_words(2)
        for g in range(PASSES):
            if g < 2:
                reorder_words(g)
            reorder_scales(g)
            first_layer(g, 0)
            first_layer(g, 1)
        for c in range(2, CHUNKS):
            for g in range(PASSES):
                first_layer(g, c)

        for tokens in first_halves:
            copy_z(tokens)
        copy_z(chunk[1])
        warm_tensor(z_bank[0], WARM_PAUSES[0])
        copy_z(chunk[2])
        for tokens in first_halves:
            make_u(tokens)
        for tokens in first_halves:
            make_pre(tokens)
        relu_on_scalar(chunk[0])
        copy_z(chunk[3])
        make_u(chunk[1])
        make_u(chunk[2])

        for c in range(2):
            make_pre(chunk[c + 1])
            relu_on_scalar(chunk[c + 1])
            if c == 1:
                make_u(chunk[3])
            second_layer(c)
            warm_tensor(z_bank[0], WARM_PAUSES[c + 1])
            bias_on_scalar(c, 0)
            bias_on_scalar(c, 1)
            store(nc.sync, c, all_tiles)

        make_pre(chunk[3])
        second_layer(2)
        relu_on_vector(chunk[3])
        second_layer(3)
        bias_on_scalar(2, 0)
        bias_on_vector(2, 1)
        store(nc.sync, 2, all_tiles)
        bias_on_vector(3, 0)
        store(nc.sync, 3, slice(0, PAIR))
        bias_on_scalar(3, 1)
        store(nc.scalar, 3, slice(PAIR, N // P))
